import numpy as np
import ml_dtypes


def mxq(x, axis, fmt="e4m3"):
    dtype, down = {"e4m3": (ml_dtypes.float8_e4m3fn, 7), "e5m2": (ml_dtypes.float8_e5m2, 14)}[fmt]
    v = np.moveaxis(np.asarray(x, np.float32).astype(ml_dtypes.bfloat16).astype(np.float64), axis, -1)
    blocks = v.reshape(v.shape[:-1] + (-1, 32))
    amax = np.abs(blocks).max(-1, keepdims=True)
    byte = np.maximum(np.where(amax > 0, np.frexp(amax)[1] - 1 + 127, 0) - down, 1)
    scale = np.exp2(byte - 127.0)
    codes = (blocks / scale).astype(np.float32).astype(dtype).astype(np.float64)
    return np.moveaxis((codes * scale).reshape(v.shape), -1, axis)


WIDE = False


def mx_kscale(k):
    if not WIDE:
        return np.ones(k)
    levels = np.array([10, -10, 5, -5, 0])
    if k % 512:
        return np.exp2(np.random.permutation(np.resize(levels, k // 32))).repeat(32)
    a = np.empty((k // 512, 16))
    for p in range(k // 512):
        a[p, :8] = np.random.permutation(np.resize(levels, 8))
        for g in range(8):
            far = levels[np.abs(levels - a[p, g]) >= 10]
            a[p, g + 8] = far[np.random.randint(len(far))]
    return np.exp2(a.ravel()).repeat(32)


def f64(x):
    return np.asarray(x).astype(np.float64)


def striped8(idx):
    return np.asarray(idx).reshape(8, -1, 16).transpose(0, 2, 1).reshape(128, -1).astype(np.uint16)


def unstriped8(offs):
    return offs.reshape(8, 16, -1).transpose(0, 2, 1).reshape(8, -1).astype(np.int64)


def pick8(x, idx, run):
    r = np.arange(len(x))
    return x[r[:, None], idx[r % (8 * run) // run]]


D, T, Q, I, G = 512, 1024, 128, 512, 64


def setup_inputs():
    n = np.random.standard_normal
    idx = np.stack([(np.random.permutation(T // 8)[:I // 8, None] * 8 + np.arange(8)).reshape(-1) for _ in range(8)])
    fd = mx_kscale(D)
    return {
        "query": (n((D, Q)) * 0.8 / np.sqrt(D) * fd[:, None]).astype(np.float32),
        "keys": (n((D, T)) / fd[:, None]).astype(np.float32),
        "offs": striped8(idx),
    }


def reference(query, keys, offs):
    idx = unstriped8(offs)
    queryq = mxq(f64(query), 0, "e4m3")
    keysq = mxq(f64(keys), 0, "e4m3")
    a = queryq.T @ keysq
    p = np.exp(pick8(a, idx, 16))
    z = p.reshape(Q, G, I // G).sum(axis=2)
    y = z / np.sum(z, axis=1, keepdims=True) * 64.0
    return y

@@ -1,0 +1,104 @@
+from contextlib import ExitStack
+
+import concourse.mybir as mybir
+
+D, T, Q, SLOTS, PAGES = 512, 1024, 128, 512, 64
+PAGE = SLOTS // PAGES
+FLOPS = 2 * D * T * Q
+
+F32 = mybir.dt.float32
+BF16 = mybir.dt.bfloat16
+U32 = mybir.dt.uint32
+U16 = mybir.dt.uint16
+U8 = mybir.dt.uint8
+FP8X4 = mybir.dt.float8_e4m3fn_x4
+ACT = mybir.ActivationFunctionType
+ALU = mybir.AluOpType
+AX = mybir.AxisListType
+
+P = 128
+PACK = 4
+CHUNKS = (256, 256, 256, 128, 128)
+HALF = SLOTS // 2
+
+
+def tile_attend_headpages_kernel(tc, query, keys, offs, out):
+    nc = tc.nc
+    with ExitStack() as ctx:
+        sb = ctx.enter_context(tc.tile_pool(name="sb", bufs=1))
+        psum = ctx.enter_context(tc.psum_pool(name="psum", bufs=1))
+
+        def load(name, rows):
+            raw = sb.tile([P, PACK, rows.shape[1]], F32, name="raw_" + name, align_bytes=64)
+            nc.sync.dma_start(out=raw[:], in_=rows.rearrange("(p j) w -> p j w", j=PACK))
+            return raw
+
+        def quantize(name, raw):
+            width = raw.shape[2]
+            split = width * 11 // 16
+            grouped = sb.tile([P, width, PACK], BF16, name="grouped_" + name, align_bytes=64)
+            codes = sb.tile([P, width], U32, name="codes_" + name, align_bytes=64)
+            scales = sb.tile([P, width], U8, name="scales_" + name, align_bytes=64)
+            nc.vector.tensor_copy(
+                out=grouped[:, :split, :].rearrange("p (c i) j -> p c j i", i=4),
+                in_=raw[:, :, :split].rearrange("p j (c i) -> p c j i", i=4),
+            )
+            nc.scalar.activation(
+                out=grouped[:, split:, :].rearrange("p (c i) j -> p c j i", i=4),
+                in_=raw[:, :, split:].rearrange("p j (c i) -> p c j i", i=4),
+                func=ACT.Copy,
+            )
+            nc.vector.quantize_mx(
+                out=codes[:].bitcast(FP8X4),
+                scales=scales[:],
+                in_=grouped[:].rearrange("p w j -> p (w j)"),
+            )
+            return codes, scales
+
+        q_raw = load("q", query)
+        starts = [sum(CHUNKS[:n]) for n in range(len(CHUNKS))]
+        k_raw = [load("k%d" % n, keys[:, s : s + w]) for n, (s, w) in enumerate(zip(starts, CHUNKS))]
+        offsets = sb.tile([P, SLOTS // 16], U16, name="offsets")
+        nc.sync.dma_start(offsets[:], offs)
+
+        q_codes, q_scales = quantize("q", q_raw)
+        scores = sb.tile([P, T], F32, name="scores", align_bytes=64)
+        for n, (s, w) in enumerate(zip(starts, CHUNKS)):
+            codes, scales = quantize("k%d" % n, k_raw[n])
+            acc = psum.tile([P, w], F32, name="acc%d" % n)
+            nc.tensor.matmul_mx(
+                out=acc[:],
+                lhsT=q_codes[:].bitcast(FP8X4),
+                lhsT_scale=q_scales[:],
+                rhs=codes[:].bitcast(FP8X4),
+                rhs_scale=scales[:],
+                start=True,
+                stop=True,
+            )
+            nc.scalar.activation(out=scores[:, s : s + w], in_=acc[:], func=ACT.Copy)
+
+        picked = sb.tile([P, SLOTS], F32, name="picked", align_bytes=64)
+        nc.vector.tensor_copy(picked[:], scores[:].indirect(offsets[:]))
+        neg_max = sb.tile([P, 1], F32, name="neg_max")
+        nc.vector.tensor_reduce(neg_max[:], picked[:], AX.X, ALU.max, negate=True)
+        weights = sb.tile([P, SLOTS], F32, name="weights", align_bytes=64)
+        sums = sb.tile([P, 2], F32, name="sums")
+        mass = sb.tile([P, PAGES], F32, name="mass")
+        for h in range(2):
+            cols = slice(h * HALF, (h + 1) * HALF)
+            nc.scalar.activation(
+                out=weights[:, cols], in_=picked[:, cols], func=ACT.Exp, bias=neg_max[:], accum_out=sums[:, h : h + 1]
+            )
+            nc.vector.tensor_reduce(
+                mass[:, h * PAGES // 2 : (h + 1) * PAGES // 2],
+                weights[:, cols].rearrange("p (g i) -> p g i", i=PAGE),
+                AX.X,
+                ALU.add,
+            )
+        total = sb.tile([P, 1], F32, name="total")
+        nc.scalar.activation(out=total[:], in_=sums[:, 0:1], func=ACT.Identity, bias=sums[:, 1:2])
+        inverse = sb.tile([P, 1], F32, name="inverse")
+        nc.vector.reciprocal(inverse[:], total[:])
+        result = sb.tile([P, PAGES], F32, name="result")
+        nc.vector.tensor_scalar(result[:], mass[:], inverse[:], float(PAGES), ALU.mult, ALU.mult)
+        nc.sync.dma_start(out=out, in_=result[:])

@@ -78,27 +78,52 @@ def tile_attend_headpages_kernel(tc, query, keys, offs, out):
             nc.scalar.activation(out=scores[:, s : s + w], in_=acc[:], func=ACT.Copy)
 
         picked = sb.tile([P, SLOTS], F32, name="picked", align_bytes=64)
-        nc.vector.tensor_copy(picked[:], scores[:].indirect(offsets[:]))
-        neg_max = sb.tile([P, 1], F32, name="neg_max")
-        nc.vector.tensor_reduce(neg_max[:], picked[:], AX.X, ALU.max, negate=True)
         weights = sb.tile([P, SLOTS], F32, name="weights", align_bytes=64)
+        neg_max = sb.tile([P, 2], F32, name="neg_max")
         sums = sb.tile([P, 2], F32, name="sums")
         mass = sb.tile([P, PAGES], F32, name="mass")
+        halves = [slice(h * HALF, (h + 1) * HALF) for h in range(2)]
+        pages = [slice(h * PAGES // 2, (h + 1) * PAGES // 2) for h in range(2)]
         for h in range(2):
-            cols = slice(h * HALF, (h + 1) * HALF)
-            nc.scalar.activation(
-                out=weights[:, cols], in_=picked[:, cols], func=ACT.Exp, bias=neg_max[:], accum_out=sums[:, h : h + 1]
+            nc.vector.tensor_copy(
+                picked[:, halves[h]], scores[:].indirect(offsets[:, h * HALF // 16 : (h + 1) * HALF // 16])
             )
+        for h in range(2):
+            nc.vector.tensor_reduce(neg_max[:, h : h + 1], picked[:, halves[h]], AX.X, ALU.max, negate=True)
+        for h in range(2):
+            nc.scalar.activation(
+                out=weights[:, halves[h]],
+                in_=picked[:, halves[h]],
+                func=ACT.Exp,
+                bias=neg_max[:, h : h + 1],
+                accum_out=sums[:, h : h + 1],
+            )
+        neg_row_max = sb.tile([P, 1], F32, name="neg_row_max")
+        nc.vector.tensor_reduce(neg_row_max[:], neg_max[:], AX.X, ALU.min)
+        factor = sb.tile([P, 2], F32, name="factor")
+        nc.scalar.activation(out=factor[:], in_=neg_max[:], func=ACT.Exp, scale=-1.0, bias=neg_row_max[:])
+
+        def page_sums(first, last):
             nc.vector.tensor_reduce(
-                mass[:, h * PAGES // 2 : (h + 1) * PAGES // 2],
-                weights[:, cols].rearrange("p (g i) -> p g i", i=PAGE),
+                mass[:, first:last],
+                weights[:, first * PAGE : last * PAGE].rearrange("p (g i) -> p g i", i=PAGE),
                 AX.X,
                 ALU.add,
             )
+
+        page_sums(0, PAGES // 2)
+        page_sums(PAGES // 2, 3 * PAGES // 4)
+        scaled_sums = sb.tile([P, 2], F32, name="scaled_sums")
         total = sb.tile([P, 1], F32, name="total")
-        nc.scalar.activation(out=total[:], in_=sums[:, 0:1], func=ACT.Identity, bias=sums[:, 1:2])
+        nc.vector.scalar_tensor_tensor(
+            scaled_sums[:], sums[:], 1.0 / PAGES, factor[:], ALU.mult, ALU.mult, accum_out=total[:]
+        )
+        page_sums(3 * PAGES // 4, PAGES)
         inverse = sb.tile([P, 1], F32, name="inverse")
         nc.vector.reciprocal(inverse[:], total[:])
         result = sb.tile([P, PAGES], F32, name="result")
-        nc.vector.tensor_scalar(result[:], mass[:], inverse[:], float(PAGES), ALU.mult, ALU.mult)
+        for h in range(2):
+            nc.vector.tensor_scalar(
+                result[:, pages[h]], mass[:, pages[h]], factor[:, h : h + 1], inverse[:], ALU.mult, ALU.mult
+            )
         nc.sync.dma_start(out=out, in_=result[:])

@@ -20,6 +20,8 @@ P = 128
 PACK = 4
 CHUNKS = (256, 256, 256, 128, 128)
 HALF = SLOTS // 2
+EARLY_PAGES = 8
+RATIO_CAP = 2.0**100
 
 
 def tile_attend_headpages_kernel(tc, query, keys, offs, out):
@@ -90,7 +92,9 @@ def tile_attend_headpages_kernel(tc, query, keys, offs, out):
             )
         for h in range(2):
             nc.vector.tensor_reduce(neg_max[:, h : h + 1], picked[:, halves[h]], AX.X, ALU.max, negate=True)
-        for h in range(2):
+        ratio = sb.tile([P, 1], F32, name="ratio")
+
+        def exponentials(h):
             nc.scalar.activation(
                 out=weights[:, halves[h]],
                 in_=picked[:, halves[h]],
@@ -98,10 +102,6 @@ def tile_attend_headpages_kernel(tc, query, keys, offs, out):
                 bias=neg_max[:, h : h + 1],
                 accum_out=sums[:, h : h + 1],
             )
-        neg_row_max = sb.tile([P, 1], F32, name="neg_row_max")
-        nc.vector.tensor_reduce(neg_row_max[:], neg_max[:], AX.X, ALU.min)
-        factor = sb.tile([P, 2], F32, name="factor")
-        nc.scalar.activation(out=factor[:], in_=neg_max[:], func=ACT.Exp, scale=-1.0, bias=neg_row_max[:])
 
         def page_sums(first, last):
             nc.vector.tensor_reduce(
@@ -111,19 +111,22 @@ def tile_attend_headpages_kernel(tc, query, keys, offs, out):
                 ALU.add,
             )
 
-        page_sums(0, PAGES // 2)
-        page_sums(PAGES // 2, 3 * PAGES // 4)
-        scaled_sums = sb.tile([P, 2], F32, name="scaled_sums")
+        exponentials(0)
+        nc.scalar.activation(out=ratio[:], in_=neg_max[:, 1:2], func=ACT.Exp, scale=-1.0, bias=neg_max[:, 0:1])
+        exponentials(1)
+        capped = sb.tile([P, 1], F32, name="capped")
+        capped_pages = sb.tile([P, 1], F32, name="capped_pages")
+        page_sums(0, EARLY_PAGES)
+        nc.vector.tensor_scalar(capped[:], ratio[:], RATIO_CAP, None, ALU.min)
+        page_sums(EARLY_PAGES, PAGES // 2)
+        page_sums(PAGES // 2, PAGES // 2 + EARLY_PAGES)
         total = sb.tile([P, 1], F32, name="total")
-        nc.vector.scalar_tensor_tensor(
-            scaled_sums[:], sums[:], 1.0 / PAGES, factor[:], ALU.mult, ALU.mult, accum_out=total[:]
-        )
-        page_sums(3 * PAGES // 4, PAGES)
+        nc.vector.tensor_scalar(total[:], sums[:, 1:2], capped[:], sums[:, 0:1], ALU.mult, ALU.add)
+        nc.vector.tensor_scalar(capped_pages[:], ratio[:], RATIO_CAP, float(PAGES), ALU.min, ALU.mult)
+        page_sums(PAGES // 2 + EARLY_PAGES, PAGES)
         inverse = sb.tile([P, 1], F32, name="inverse")
         nc.vector.reciprocal(inverse[:], total[:])
         result = sb.tile([P, PAGES], F32, name="result")
-        for h in range(2):
-            nc.vector.tensor_scalar(
-                result[:, pages[h]], mass[:, pages[h]], factor[:, h : h + 1], inverse[:], ALU.mult, ALU.mult
-            )
+        nc.vector.tensor_scalar(result[:, pages[0]], mass[:, pages[0]], inverse[:], float(PAGES), ALU.mult, ALU.mult)
+        nc.vector.tensor_scalar(result[:, pages[1]], mass[:, pages[1]], inverse[:], capped_pages[:], ALU.mult, ALU.mult)
         nc.sync.dma_start(out=out, in_=result[:])

@@ -83,7 +83,8 @@ def tile_attend_headpages_kernel(tc, query, keys, offs, out):
         weights = sb.tile([P, SLOTS], F32, name="weights", align_bytes=64)
         neg_max = sb.tile([P, 2], F32, name="neg_max")
         sums = sb.tile([P, 2], F32, name="sums")
-        mass = sb.tile([P, PAGES], F32, name="mass")
+        early_mass = sb.tile([P, PAGES // 2], F32, name="early_mass")
+        mass = picked[:, HALF : HALF + PAGES]
         halves = [slice(h * HALF, (h + 1) * HALF) for h in range(2)]
         pages = [slice(h * PAGES // 2, (h + 1) * PAGES // 2) for h in range(2)]
         for h in range(2):
@@ -105,28 +106,26 @@ def tile_attend_headpages_kernel(tc, query, keys, offs, out):
 
         def page_sums(first, last):
             nc.vector.tensor_reduce(
-                mass[:, first:last],
+                (early_mass if first < PAGES // 2 else mass)[:, first:last],
                 weights[:, first * PAGE : last * PAGE].rearrange("p (g i) -> p g i", i=PAGE),
                 AX.X,
                 ALU.add,
             )
 
         exponentials(0)
-        nc.scalar.activation(out=ratio[:], in_=neg_max[:, 1:2], func=ACT.Exp, scale=-1.0, bias=neg_max[:, 0:1])
+        nc.scalar.activation(out=ratio[:], in_=neg_max[:, 0:1], func=ACT.Exp, scale=-1.0, bias=neg_max[:, 1:2])
         exponentials(1)
         capped = sb.tile([P, 1], F32, name="capped")
-        capped_pages = sb.tile([P, 1], F32, name="capped_pages")
         page_sums(0, EARLY_PAGES)
         nc.vector.tensor_scalar(capped[:], ratio[:], RATIO_CAP, None, ALU.min)
         page_sums(EARLY_PAGES, PAGES // 2)
         page_sums(PAGES // 2, PAGES // 2 + EARLY_PAGES)
         total = sb.tile([P, 1], F32, name="total")
-        nc.vector.tensor_scalar(total[:], sums[:, 1:2], capped[:], sums[:, 0:1], ALU.mult, ALU.add)
-        nc.vector.tensor_scalar(capped_pages[:], ratio[:], RATIO_CAP, float(PAGES), ALU.min, ALU.mult)
+        nc.vector.tensor_scalar(total[:], sums[:, 0:1], capped[:], sums[:, 1:2], ALU.mult, ALU.add)
         page_sums(PAGES // 2 + EARLY_PAGES, PAGES)
         inverse = sb.tile([P, 1], F32, name="inverse")
+        nc.vector.tensor_scalar(mass[:, pages[0]], early_mass[:], capped[:], None, ALU.mult)
         nc.vector.reciprocal(inverse[:], total[:])
         result = sb.tile([P, PAGES], F32, name="result")
-        nc.vector.tensor_scalar(result[:, pages[0]], mass[:, pages[0]], inverse[:], float(PAGES), ALU.mult, ALU.mult)
-        nc.vector.tensor_scalar(result[:, pages[1]], mass[:, pages[1]], inverse[:], capped_pages[:], ALU.mult, ALU.mult)
+        nc.vector.tensor_scalar(result[:], mass, inverse[:], float(PAGES), ALU.mult, ALU.mult)
         nc.sync.dma_start(out=out, in_=result[:])

@@ -31,7 +31,7 @@ def tile_attend_headpages_kernel(tc, query, keys, offs, out):
         psum = ctx.enter_context(tc.psum_pool(name="psum", bufs=1))
 
         def load(name, rows):
-            raw = sb.tile([P, PACK, rows.shape[1]], F32, name="raw_" + name, align_bytes=64)
+            raw = sb.tile([P, PACK, rows.shape[1]], F32, name="raw_" + name, align_bytes=256)
             nc.sync.dma_start(out=raw[:], in_=rows.rearrange("(p j) w -> p j w", j=PACK))
             return raw
 
@@ -126,6 +126,6 @@ def tile_attend_headpages_kernel(tc, query, keys, offs, out):
         inverse = sb.tile([P, 1], F32, name="inverse")
         nc.vector.tensor_scalar(mass[:, pages[0]], early_mass[:], capped[:], None, ALU.mult)
         nc.vector.reciprocal(inverse[:], total[:])
-        result = sb.tile([P, PAGES], F32, name="result")
+        result = sb.tile([P, PAGES], F32, name="result", align_bytes=256)
         nc.vector.tensor_scalar(result[:], mass, inverse[:], float(PAGES), ALU.mult, ALU.mult)
         nc.sync.dma_start(out=out, in_=result[:])

@@ -19,6 +19,8 @@ AX = mybir.AxisListType
 P = 128
 PACK = 4
 CHUNKS = (256, 256, 256, 128, 128)
+VECTOR_SHARE = {"k3": 32, "k4": 96}
+STAGED_IN_SCORES = {"k3": 0, "k4": T // 2}
 HALF = SLOTS // 2
 EARLY_PAGES = 8
 RATIO_CAP = 2.0**100
@@ -30,14 +32,21 @@ def tile_attend_headpages_kernel(tc, query, keys, offs, out):
         sb = ctx.enter_context(tc.tile_pool(name="sb", bufs=1))
         psum = ctx.enter_context(tc.psum_pool(name="psum", bufs=1))
 
+        scores = sb.tile([P, T], F32, name="scores", align_bytes=256)
+
         def load(name, rows):
-            raw = sb.tile([P, PACK, rows.shape[1]], F32, name="raw_" + name, align_bytes=256)
-            nc.sync.dma_start(out=raw[:], in_=rows.rearrange("(p j) w -> p j w", j=PACK))
+            if name in STAGED_IN_SCORES:
+                first = STAGED_IN_SCORES[name]
+                raw = scores[:, first : first + T // 2].rearrange("p (j w) -> p j w", j=PACK)
+            else:
+                tile = sb.tile([P, PACK, rows.shape[1]], F32, name="raw_" + name, align_bytes=256)
+                raw = tile[:]
+            nc.sync.dma_start(out=raw, in_=rows.rearrange("(p j) w -> p j w", j=PACK))
             return raw
 
         def quantize(name, raw):
             width = raw.shape[2]
-            split = width * 11 // 16
+            split = VECTOR_SHARE.get(name, width * 11 // 16)
             grouped = sb.tile([P, width, PACK], BF16, name="grouped_" + name, align_bytes=64)
             codes = sb.tile([P, width], U32, name="codes_" + name, align_bytes=64)
             scales = sb.tile([P, width], U8, name="scales_" + name, align_bytes=64)
@@ -64,7 +73,7 @@ def tile_attend_headpages_kernel(tc, query, keys, offs, out):
         nc.sync.dma_start(offsets[:], offs)
 
         q_codes, q_scales = quantize("q", q_raw)
-        scores = sb.tile([P, T], F32, name="scores", align_bytes=64)
+        banks = []
         for n, (s, w) in enumerate(zip(starts, CHUNKS)):
             codes, scales = quantize("k%d" % n, k_raw[n])
             acc = psum.tile([P, w], F32, name="acc%d" % n)
@@ -77,7 +86,12 @@ def tile_attend_headpages_kernel(tc, query, keys, offs, out):
                 start=True,
                 stop=True,
             )
-            nc.scalar.activation(out=scores[:, s : s + w], in_=acc[:], func=ACT.Copy)
+            banks.append(acc)
+        for n, (acc, s, w) in enumerate(zip(banks, starts, CHUNKS)):
+            if n == 2:
+                nc.vector.tensor_copy(out=scores[:, s : s + w], in_=acc[:])
+            else:
+                nc.scalar.activation(out=scores[:, s : s + w], in_=acc[:], func=ACT.Copy)
 
         picked = sb.tile([P, SLOTS], F32, name="picked", align_bytes=64)
         weights = sb.tile([P, SLOTS], F32, name="weights", align_bytes=64)

@@ -20,7 +20,7 @@ P = 128
 PACK = 4
 CHUNKS = (256, 256, 256, 128, 128)
 VECTOR_SHARE = {"k3": 32, "k4": 96}
-STAGED_IN_SCORES = {"k3": 0, "k4": T // 2}
+STAGED_IN_SCORES = ("k4",)
 HALF = SLOTS // 2
 EARLY_PAGES = 8
 RATIO_CAP = 2.0**100
@@ -36,8 +36,7 @@ def tile_attend_headpages_kernel(tc, query, keys, offs, out):
 
         def load(name, rows):
             if name in STAGED_IN_SCORES:
-                first = STAGED_IN_SCORES[name]
-                raw = scores[:, first : first + T // 2].rearrange("p (j w) -> p j w", j=PACK)
+                raw = scores[:, 384:896].rearrange("p (j w) -> p j w", j=PACK)
             else:
                 tile = sb.tile([P, PACK, rows.shape[1]], F32, name="raw_" + name, align_bytes=256)
                 raw = tile[:]
@@ -87,10 +86,12 @@ def tile_attend_headpages_kernel(tc, query, keys, offs, out):
                 stop=True,
             )
             banks.append(acc)
+            if n == 0:
+                nc.scalar.activation(out=scores[:, s : s + w], in_=acc[:], func=ACT.Copy)
         for n, (acc, s, w) in enumerate(zip(banks, starts, CHUNKS)):
-            if n == 2:
+            if n == 3:
                 nc.vector.tensor_copy(out=scores[:, s : s + w], in_=acc[:])
-            else:
+            elif n:
                 nc.scalar.activation(out=scores[:, s : s + w], in_=acc[:], func=ACT.Copy)
 
         picked = sb.tile([P, SLOTS], F32, name="picked", align_bytes=64)

@@ -46,9 +46,9 @@ def tile_attend_headpages_kernel(tc, query, keys, offs, out):
         def quantize(name, raw):
             width = raw.shape[2]
             split = VECTOR_SHARE.get(name, width * 11 // 16)
-            grouped = sb.tile([P, width, PACK], BF16, name="grouped_" + name, align_bytes=64)
-            codes = sb.tile([P, width], U32, name="codes_" + name, align_bytes=64)
-            scales = sb.tile([P, width], U8, name="scales_" + name, align_bytes=64)
+            grouped = sb.tile([P, width, PACK], BF16, name="grouped_" + name, align_bytes=256)
+            codes = sb.tile([P, width], U32, name="codes_" + name, align_bytes=256)
+            scales = sb.tile([P, width], U8, name="scales_" + name, align_bytes=256)
             nc.vector.tensor_copy(
                 out=grouped[:, :split, :].rearrange("p (c i) j -> p c j i", i=4),
                 in_=raw[:, :, :split].rearrange("p j (c i) -> p c j i", i=4),
@@ -94,8 +94,8 @@ def tile_attend_headpages_kernel(tc, query, keys, offs, out):
             elif n:
                 nc.scalar.activation(out=scores[:, s : s + w], in_=acc[:], func=ACT.Copy)
 
-        picked = sb.tile([P, SLOTS], F32, name="picked", align_bytes=64)
-        weights = sb.tile([P, SLOTS], F32, name="weights", align_bytes=64)
+        picked = sb.tile([P, SLOTS], F32, name="picked", align_bytes=256)
+        weights = sb.tile([P, SLOTS], F32, name="weights", align_bytes=256)
         neg_max = sb.tile([P, 2], F32, name="neg_max")
         sums = sb.tile([P, 2], F32, name="sums")
         early_mass = sb.tile([P, PAGES // 2], F32, name="early_mass")

@@ -19,7 +19,6 @@ AX = mybir.AxisListType
 P = 128
 PACK = 4
 CHUNKS = (256, 256, 256, 128, 128)
-VECTOR_SHARE = {"k3": 32, "k4": 96}
 STAGED_IN_SCORES = ("k4",)
 HALF = SLOTS // 2
 EARLY_PAGES = 8
@@ -43,27 +42,40 @@ def tile_attend_headpages_kernel(tc, query, keys, offs, out):
             nc.sync.dma_start(out=raw, in_=rows.rearrange("(p j) w -> p j w", j=PACK))
             return raw
 
-        def quantize(name, raw):
-            width = raw.shape[2]
-            split = VECTOR_SHARE.get(name, width * 11 // 16)
-            grouped = sb.tile([P, width, PACK], BF16, name="grouped_" + name, align_bytes=256)
-            codes = sb.tile([P, width], U32, name="codes_" + name, align_bytes=256)
-            scales = sb.tile([P, width], U8, name="scales_" + name, align_bytes=256)
+        def interleave(grouped, raw, first, split, last):
+            if split > first:
+                on_vector(grouped, raw, first, split)
+            if last > split:
+                on_scalar(grouped, raw, split, last)
+
+        def on_vector(grouped, raw, first, split):
             nc.vector.tensor_copy(
-                out=grouped[:, :split, :].rearrange("p (c i) j -> p c j i", i=4),
-                in_=raw[:, :, :split].rearrange("p j (c i) -> p c j i", i=4),
+                out=grouped[:, first:split, :].rearrange("p (c i) j -> p c j i", i=4),
+                in_=raw[:, :, first:split].rearrange("p j (c i) -> p c j i", i=4),
             )
+
+        def on_scalar(grouped, raw, split, last):
             nc.scalar.activation(
-                out=grouped[:, split:, :].rearrange("p (c i) j -> p c j i", i=4),
-                in_=raw[:, :, split:].rearrange("p j (c i) -> p c j i", i=4),
+                out=grouped[:, split:last, :].rearrange("p (c i) j -> p c j i", i=4),
+                in_=raw[:, :, split:last].rearrange("p j (c i) -> p c j i", i=4),
                 func=ACT.Copy,
             )
-            nc.vector.quantize_mx(
-                out=codes[:].bitcast(FP8X4),
-                scales=scales[:],
-                in_=grouped[:].rearrange("p w j -> p (w j)"),
-            )
+
+        def quantize(name, grouped, first, last, pieces=1):
+            width = last - first
+            codes = sb.tile([P, width], U32, name="codes_" + name, align_bytes=256)
+            scales = sb.tile([P, width], U8, name="scales_" + name, align_bytes=256)
+            step = width // pieces
+            for c in range(0, width, step):
+                nc.vector.quantize_mx(
+                    out=codes[:, c : c + step].bitcast(FP8X4),
+                    scales=scales[:, c : c + step],
+                    in_=grouped[:, first + c : first + c + step, :].rearrange("p w j -> p (w j)"),
+                )
             return codes, scales
+
+        def grouped_tile(name, width):
+            return sb.tile([P, width, PACK], BF16, name="grouped_" + name, align_bytes=256)
 
         q_raw = load("q", query)
         starts = [sum(CHUNKS[:n]) for n in range(len(CHUNKS))]
@@ -71,11 +83,13 @@ def tile_attend_headpages_kernel(tc, query, keys, offs, out):
         offsets = sb.tile([P, SLOTS // 16], U16, name="offsets")
         nc.sync.dma_start(offsets[:], offs)
 
-        q_codes, q_scales = quantize("q", q_raw)
-        banks = []
-        for n, (s, w) in enumerate(zip(starts, CHUNKS)):
-            codes, scales = quantize("k%d" % n, k_raw[n])
-            acc = psum.tile([P, w], F32, name="acc%d" % n)
+        q_grouped = grouped_tile("q", Q)
+        interleave(q_grouped, q_raw, 0, 88, Q)
+        q_codes, q_scales = quantize("q", q_grouped, 0, Q)
+
+        def multiply(name, grouped, first, last, column, pieces=1):
+            codes, scales = quantize(name, grouped, first, last, pieces)
+            acc = psum.tile([P, last - first], F32, name="acc_" + name)
             nc.tensor.matmul_mx(
                 out=acc[:],
                 lhsT=q_codes[:].bitcast(FP8X4),
@@ -85,14 +99,34 @@ def tile_attend_headpages_kernel(tc, query, keys, offs, out):
                 start=True,
                 stop=True,
             )
-            banks.append(acc)
+            return acc, slice(column + first, column + last)
+
+        def empty(bank, by_vector=False):
+            acc, columns = bank
+            if by_vector:
+                nc.vector.tensor_copy(out=scores[:, columns], in_=acc[:])
+            else:
+                nc.scalar.activation(out=scores[:, columns], in_=acc[:], func=ACT.Copy)
+
+        g = [grouped_tile("k%d" % n, w) for n, w in enumerate(CHUNKS)]
+        banks = []
+        for n in range(3):
+            interleave(g[n], k_raw[n], 0, 128, 128)
+            interleave(g[n], k_raw[n], 128, 176, 256)
+            banks.append(multiply("k%d" % n, g[n], 0, 256, starts[n], 2))
             if n == 0:
-                nc.scalar.activation(out=scores[:, s : s + w], in_=acc[:], func=ACT.Copy)
-        for n, (acc, s, w) in enumerate(zip(banks, starts, CHUNKS)):
-            if n == 3:
-                nc.vector.tensor_copy(out=scores[:, s : s + w], in_=acc[:])
-            elif n:
-                nc.scalar.activation(out=scores[:, s : s + w], in_=acc[:], func=ACT.Copy)
+                empty(banks[0])
+        interleave(g[3], k_raw[3], 0, 32, 128)
+        interleave(g[4], k_raw[4], 0, 64, 64)
+        interleave(g[4], k_raw[4], 64, 88, 128)
+        banks.append(multiply("k3", g[3], 0, 128, starts[3]))
+        banks.append(multiply("k4a", g[4], 0, 64, starts[4]))
+        banks.append(multiply("k4b", g[4], 64, 128, starts[4]))
+        empty(banks[1])
+        empty(banks[2])
+        empty(banks[3], by_vector=True)
+        empty(banks[4], by_vector=True)
+        empty(banks[5])
 
         picked = sb.tile([P, SLOTS], F32, name="picked", align_bytes=256)
         weights = sb.tile([P, SLOTS], F32, name="weights", align_bytes=256)

@@ -18,11 +18,19 @@ AX = mybir.AxisListType
 
 P = 128
 PACK = 4
-CHUNKS = (256, 256, 256, 128, 128)
-STAGED_IN_SCORES = ("k4",)
+RUN = 4
+ALIGN = 256
+LIST_ROWS = 16
+
+WIDE, NARROW = 256, 128
+LOADS = (WIDE, WIDE, WIDE, NARROW, NARROW)
+VECTOR_OF_QUERY, VECTOR_OF_WIDE, VECTOR_OF_FOURTH, VECTOR_OF_LAST = 88, 176, 32, 80
+STAGING = slice(384, 896)
+
 HALF = SLOTS // 2
+HALF_PAGES = PAGES // 2
 EARLY_PAGES = 8
-RATIO_CAP = 2.0**100
+GAP_CAP = 64.0
 
 
 def tile_attend_headpages_kernel(tc, query, keys, offs, out):
@@ -31,40 +39,33 @@ def tile_attend_headpages_kernel(tc, query, keys, offs, out):
         sb = ctx.enter_context(tc.tile_pool(name="sb", bufs=1))
         psum = ctx.enter_context(tc.psum_pool(name="psum", bufs=1))
 
-        scores = sb.tile([P, T], F32, name="scores", align_bytes=256)
+        scores = sb.tile([P, T], F32, name="scores", align_bytes=ALIGN)
 
-        def load(name, rows):
-            if name in STAGED_IN_SCORES:
-                raw = scores[:, 384:896].rearrange("p (j w) -> p j w", j=PACK)
-            else:
-                tile = sb.tile([P, PACK, rows.shape[1]], F32, name="raw_" + name, align_bytes=256)
-                raw = tile[:]
+        def staging_tile(name, width):
+            return sb.tile([P, PACK, width], F32, name="raw_" + name, align_bytes=ALIGN)[:]
+
+        def load(raw, rows):
             nc.sync.dma_start(out=raw, in_=rows.rearrange("(p j) w -> p j w", j=PACK))
             return raw
 
-        def interleave(grouped, raw, first, split, last):
-            if split > first:
-                on_vector(grouped, raw, first, split)
-            if last > split:
-                on_scalar(grouped, raw, split, last)
+        def grouped_tile(name, width):
+            return sb.tile([P, width, PACK], BF16, name="grouped_" + name, align_bytes=ALIGN)
 
-        def on_vector(grouped, raw, first, split):
-            nc.vector.tensor_copy(
-                out=grouped[:, first:split, :].rearrange("p (c i) j -> p c j i", i=4),
-                in_=raw[:, :, first:split].rearrange("p j (c i) -> p c j i", i=4),
+        def interleaving_views(grouped, raw, first, last):
+            return dict(
+                out=grouped[:, first:last, :].rearrange("p (c i) j -> p c j i", i=RUN),
+                in_=raw[:, :, first:last].rearrange("p j (c i) -> p c j i", i=RUN),
             )
 
-        def on_scalar(grouped, raw, split, last):
-            nc.scalar.activation(
-                out=grouped[:, split:last, :].rearrange("p (c i) j -> p c j i", i=4),
-                in_=raw[:, :, split:last].rearrange("p j (c i) -> p c j i", i=4),
-                func=ACT.Copy,
-            )
+        def interleave(grouped, raw, vector_cuts):
+            for first, last in zip((0,) + vector_cuts, vector_cuts):
+                nc.vector.tensor_copy(**interleaving_views(grouped, raw, first, last))
+            nc.scalar.activation(func=ACT.Copy, **interleaving_views(grouped, raw, vector_cuts[-1], raw.shape[2]))
 
         def quantize(name, grouped, first, last, pieces=1):
             width = last - first
-            codes = sb.tile([P, width], U32, name="codes_" + name, align_bytes=256)
-            scales = sb.tile([P, width], U8, name="scales_" + name, align_bytes=256)
+            codes = sb.tile([P, width], U32, name="codes_" + name, align_bytes=ALIGN)
+            scales = sb.tile([P, width], U8, name="scales_" + name, align_bytes=ALIGN)
             step = width // pieces
             for c in range(0, width, step):
                 nc.vector.quantize_mx(
@@ -74,21 +75,24 @@ def tile_attend_headpages_kernel(tc, query, keys, offs, out):
                 )
             return codes, scales
 
-        def grouped_tile(name, width):
-            return sb.tile([P, width, PACK], BF16, name="grouped_" + name, align_bytes=256)
-
-        q_raw = load("q", query)
-        starts = [sum(CHUNKS[:n]) for n in range(len(CHUNKS))]
-        k_raw = [load("k%d" % n, keys[:, s : s + w]) for n, (s, w) in enumerate(zip(starts, CHUNKS))]
-        offsets = sb.tile([P, SLOTS // 16], U16, name="offsets")
+        starts = [sum(LOADS[:n]) for n in range(len(LOADS))]
+        q_raw = load(staging_tile("q", Q), query)
+        k_raw = [
+            load(staging_tile("k%d" % n, w), keys[:, s : s + w])
+            for n, (s, w) in enumerate(zip(starts[:-1], LOADS[:-1]))
+        ]
+        k_raw.append(load(scores[:, STAGING].rearrange("p (j w) -> p j w", j=PACK), keys[:, starts[-1] :]))
+        offsets = sb.tile([P, SLOTS // LIST_ROWS], U16, name="offsets")
         nc.sync.dma_start(offsets[:], offs)
 
         q_grouped = grouped_tile("q", Q)
-        interleave(q_grouped, q_raw, 0, 88, Q)
+        interleave(q_grouped, q_raw, (VECTOR_OF_QUERY,))
         q_codes, q_scales = quantize("q", q_grouped, 0, Q)
 
-        def multiply(name, grouped, first, last, column, pieces=1):
-            codes, scales = quantize(name, grouped, first, last, pieces)
+        k_grouped = [grouped_tile("k%d" % n, w) for n, w in enumerate(LOADS)]
+
+        def multiply(name, n, first, last, pieces=1):
+            codes, scales = quantize(name, k_grouped[n], first, last, pieces)
             acc = psum.tile([P, last - first], F32, name="acc_" + name)
             nc.tensor.matmul_mx(
                 out=acc[:],
@@ -99,50 +103,51 @@ def tile_attend_headpages_kernel(tc, query, keys, offs, out):
                 start=True,
                 stop=True,
             )
-            return acc, slice(column + first, column + last)
+            return acc, slice(starts[n] + first, starts[n] + last)
 
-        def empty(bank, by_vector=False):
+        def empty_on_scalar(bank):
             acc, columns = bank
-            if by_vector:
-                nc.vector.tensor_copy(out=scores[:, columns], in_=acc[:])
-            else:
-                nc.scalar.activation(out=scores[:, columns], in_=acc[:], func=ACT.Copy)
+            nc.scalar.activation(out=scores[:, columns], in_=acc[:], func=ACT.Copy)
 
-        g = [grouped_tile("k%d" % n, w) for n, w in enumerate(CHUNKS)]
-        banks = []
-        for n in range(3):
-            interleave(g[n], k_raw[n], 0, 128, 128)
-            interleave(g[n], k_raw[n], 128, 176, 256)
-            banks.append(multiply("k%d" % n, g[n], 0, 256, starts[n], 2))
-            if n == 0:
-                empty(banks[0])
-        interleave(g[3], k_raw[3], 0, 32, 128)
-        interleave(g[4], k_raw[4], 0, 64, 64)
-        interleave(g[4], k_raw[4], 64, 88, 128)
-        banks.append(multiply("k3", g[3], 0, 128, starts[3]))
-        banks.append(multiply("k4a", g[4], 0, 64, starts[4]))
-        banks.append(multiply("k4b", g[4], 64, 128, starts[4]))
-        empty(banks[1])
-        empty(banks[2])
-        empty(banks[3], by_vector=True)
-        empty(banks[4], by_vector=True)
-        empty(banks[5])
+        def empty_on_vector(bank):
+            acc, columns = bank
+            nc.vector.tensor_copy(out=scores[:, columns], in_=acc[:])
 
-        picked = sb.tile([P, SLOTS], F32, name="picked", align_bytes=256)
-        weights = sb.tile([P, SLOTS], F32, name="weights", align_bytes=256)
+        def wide_load(n):
+            interleave(k_grouped[n], k_raw[n], (WIDE // 2, VECTOR_OF_WIDE))
+            return multiply("k%d" % n, n, 0, WIDE, pieces=2)
+
+        empty_on_scalar(wide_load(0))
+        second_bank = wide_load(1)
+        third_bank = wide_load(2)
+        interleave(k_grouped[3], k_raw[3], (VECTOR_OF_FOURTH,))
+        interleave(k_grouped[4], k_raw[4], (NARROW // 2, VECTOR_OF_LAST))
+        fourth_bank = multiply("k3", 3, 0, NARROW)
+        fifth_bank = multiply("k4a", 4, 0, NARROW // 2)
+        sixth_bank = multiply("k4b", 4, NARROW // 2, NARROW)
+        empty_on_scalar(second_bank)
+        empty_on_scalar(third_bank)
+        empty_on_vector(fourth_bank)
+        empty_on_vector(fifth_bank)
+        empty_on_scalar(sixth_bank)
+
+        picked = sb.tile([P, SLOTS], F32, name="picked", align_bytes=ALIGN)
+        weights = sb.tile([P, SLOTS], F32, name="weights", align_bytes=ALIGN)
         neg_max = sb.tile([P, 2], F32, name="neg_max")
         sums = sb.tile([P, 2], F32, name="sums")
-        early_mass = sb.tile([P, PAGES // 2], F32, name="early_mass")
-        mass = picked[:, HALF : HALF + PAGES]
+        early_mass = sb.tile([P, HALF_PAGES], F32, name="early_mass")
         halves = [slice(h * HALF, (h + 1) * HALF) for h in range(2)]
-        pages = [slice(h * PAGES // 2, (h + 1) * PAGES // 2) for h in range(2)]
         for h in range(2):
-            nc.vector.tensor_copy(
-                picked[:, halves[h]], scores[:].indirect(offsets[:, h * HALF // 16 : (h + 1) * HALF // 16])
-            )
+            listed = offsets[:, h * HALF // LIST_ROWS : (h + 1) * HALF // LIST_ROWS]
+            nc.vector.tensor_copy(picked[:, halves[h]], scores[:].indirect(listed))
         for h in range(2):
             nc.vector.tensor_reduce(neg_max[:, h : h + 1], picked[:, halves[h]], AX.X, ALU.max, negate=True)
         ratio = sb.tile([P, 1], F32, name="ratio")
+        total = sb.tile([P, 1], F32, name="total")
+        inverse = sb.tile([P, 1], F32, name="inverse")
+        result = sb.tile([P, PAGES], F32, name="result", align_bytes=ALIGN)
+        mass = sb.tile([P, PAGES], F32, name="mass", align_bytes=ALIGN)
+        gap = mass[:, PAGES - 1 :]
 
         def exponentials(h):
             nc.scalar.activation(
@@ -153,28 +158,23 @@ def tile_attend_headpages_kernel(tc, query, keys, offs, out):
                 accum_out=sums[:, h : h + 1],
             )
 
-        def page_sums(first, last):
+        def page_sums(masses, first, last):
             nc.vector.tensor_reduce(
-                (early_mass if first < PAGES // 2 else mass)[:, first:last],
+                masses[:, first:last],
                 weights[:, first * PAGE : last * PAGE].rearrange("p (g i) -> p g i", i=PAGE),
                 AX.X,
                 ALU.add,
             )
 
         exponentials(0)
-        nc.scalar.activation(out=ratio[:], in_=neg_max[:, 0:1], func=ACT.Exp, scale=-1.0, bias=neg_max[:, 1:2])
+        nc.vector.tensor_scalar(gap, neg_max[:, 1:2], neg_max[:, 0:1], GAP_CAP, ALU.subtract, ALU.min)
         exponentials(1)
-        capped = sb.tile([P, 1], F32, name="capped")
-        page_sums(0, EARLY_PAGES)
-        nc.vector.tensor_scalar(capped[:], ratio[:], RATIO_CAP, None, ALU.min)
-        page_sums(EARLY_PAGES, PAGES // 2)
-        page_sums(PAGES // 2, PAGES // 2 + EARLY_PAGES)
-        total = sb.tile([P, 1], F32, name="total")
-        nc.vector.tensor_scalar(total[:], sums[:, 0:1], capped[:], sums[:, 1:2], ALU.mult, ALU.add)
-        page_sums(PAGES // 2 + EARLY_PAGES, PAGES)
-        inverse = sb.tile([P, 1], F32, name="inverse")
-        nc.vector.tensor_scalar(mass[:, pages[0]], early_mass[:], capped[:], None, ALU.mult)
+        nc.scalar.activation(out=ratio[:], in_=gap, func=ACT.Exp)
+        page_sums(early_mass, 0, HALF_PAGES)
+        page_sums(mass, HALF_PAGES, HALF_PAGES + EARLY_PAGES)
+        nc.vector.tensor_scalar(total[:], sums[:, 0:1], ratio[:], sums[:, 1:2], ALU.mult, ALU.add)
+        page_sums(mass, HALF_PAGES + EARLY_PAGES, PAGES)
+        nc.vector.tensor_scalar(mass[:, :HALF_PAGES], early_mass[:], ratio[:], None, ALU.mult)
         nc.vector.reciprocal(inverse[:], total[:])
-        result = sb.tile([P, PAGES], F32, name="result", align_bytes=256)
-        nc.vector.tensor_scalar(result[:], mass, inverse[:], float(PAGES), ALU.mult, ALU.mult)
+        nc.vector.tensor_scalar(result[:], mass[:], inverse[:], float(PAGES), ALU.mult, ALU.mult)
         nc.sync.dma_start(out=out, in_=result[:])

@@ -137,9 +137,9 @@ def tile_attend_headpages_kernel(tc, query, keys, offs, out):
         sums = sb.tile([P, 2], F32, name="sums")
         early_mass = sb.tile([P, HALF_PAGES], F32, name="early_mass")
         halves = [slice(h * HALF, (h + 1) * HALF) for h in range(2)]
-        for h in range(2):
-            listed = offsets[:, h * HALF // LIST_ROWS : (h + 1) * HALF // LIST_ROWS]
-            nc.vector.tensor_copy(picked[:, halves[h]], scores[:].indirect(listed))
+        listed = [offsets[:, h * HALF // LIST_ROWS : (h + 1) * HALF // LIST_ROWS] for h in range(2)]
+        nc.vector.tensor_copy(picked[:, halves[0]], scores[:].indirect(listed[0]))
+        nc.scalar.activation(out=picked[:, halves[1]], in_=scores[:].indirect(listed[1]), func=ACT.Copy)
         for h in range(2):
             nc.vector.tensor_reduce(neg_max[:, h : h + 1], picked[:, halves[h]], AX.X, ALU.max, negate=True)
         ratio = sb.tile([P, 1], F32, name="ratio")

@@ -27,6 +27,7 @@ LOADS = (WIDE, WIDE, WIDE, NARROW, NARROW)
 VECTOR_OF_QUERY, VECTOR_OF_WIDE, VECTOR_OF_FOURTH, VECTOR_OF_LAST = 88, 176, 32, 80
 STAGING = slice(384, 896)
 
+VECTOR_OF_THIRD = 144
 HALF = SLOTS // 2
 HALF_PAGES = PAGES // 2
 EARLY_PAGES = 8
@@ -113,13 +114,13 @@ def tile_attend_headpages_kernel(tc, query, keys, offs, out):
             acc, columns = bank
             nc.vector.tensor_copy(out=scores[:, columns], in_=acc[:])
 
-        def wide_load(n):
-            interleave(k_grouped[n], k_raw[n], (WIDE // 2, VECTOR_OF_WIDE))
+        def wide_load(n, share):
+            interleave(k_grouped[n], k_raw[n], (WIDE // 2, share))
             return multiply("k%d" % n, n, 0, WIDE, pieces=2)
 
-        empty_on_scalar(wide_load(0))
-        second_bank = wide_load(1)
-        third_bank = wide_load(2)
+        empty_on_scalar(wide_load(0, VECTOR_OF_WIDE))
+        second_bank = wide_load(1, VECTOR_OF_WIDE)
+        third_bank = wide_load(2, VECTOR_OF_THIRD)
         interleave(k_grouped[3], k_raw[3], (VECTOR_OF_FOURTH,))
         interleave(k_grouped[4], k_raw[4], (NARROW // 2, VECTOR_OF_LAST))
         fourth_bank = multiply("k3", 3, 0, NARROW)

@@ -135,47 +135,44 @@ def tile_attend_headpages_kernel(tc, query, keys, offs, out):
         picked = sb.tile([P, SLOTS], F32, name="picked", align_bytes=ALIGN)
         weights = sb.tile([P, SLOTS], F32, name="weights", align_bytes=ALIGN)
         neg_max = sb.tile([P, 2], F32, name="neg_max")
-        sums = sb.tile([P, 2], F32, name="sums")
-        early_mass = sb.tile([P, HALF_PAGES], F32, name="early_mass")
+        neg_shift = sb.tile([P, 1], F32, name="neg_shift")
+        stats = sb.tile([P, 9], F32, name="stats")
+        inverse = sb.tile([P, 2], F32, name="inverse")
+        result = sb.tile([P, PAGES], F32, name="result", align_bytes=ALIGN)
+        mass = sb.tile([P, PAGES], F32, name="mass", align_bytes=ALIGN)
+        nc.gpsimd.memset(stats[:], 0.0)
         halves = [slice(h * HALF, (h + 1) * HALF) for h in range(2)]
         listed = [offsets[:, h * HALF // LIST_ROWS : (h + 1) * HALF // LIST_ROWS] for h in range(2)]
         nc.vector.tensor_copy(picked[:, halves[0]], scores[:].indirect(listed[0]))
         nc.scalar.activation(out=picked[:, halves[1]], in_=scores[:].indirect(listed[1]), func=ACT.Copy)
         for h in range(2):
             nc.vector.tensor_reduce(neg_max[:, h : h + 1], picked[:, halves[h]], AX.X, ALU.max, negate=True)
-        ratio = sb.tile([P, 1], F32, name="ratio")
-        total = sb.tile([P, 1], F32, name="total")
-        inverse = sb.tile([P, 1], F32, name="inverse")
-        result = sb.tile([P, PAGES], F32, name="result", align_bytes=ALIGN)
-        mass = sb.tile([P, PAGES], F32, name="mass", align_bytes=ALIGN)
-        gap = mass[:, PAGES - 1 :]
+        nc.vector.tensor_scalar(neg_shift[:], neg_max[:, 1:2], GAP_CAP, neg_max[:, 0:1], ALU.add, ALU.min)
 
-        def exponentials(h):
+        def exponentials(first, last, bias, total):
             nc.scalar.activation(
-                out=weights[:, halves[h]],
-                in_=picked[:, halves[h]],
+                out=weights[:, first * PAGE : last * PAGE],
+                in_=picked[:, first * PAGE : last * PAGE],
                 func=ACT.Exp,
-                bias=neg_max[:, h : h + 1],
-                accum_out=sums[:, h : h + 1],
+                bias=bias,
+                accum_out=total,
             )
 
-        def page_sums(masses, first, last):
+        def page_sums(first, last):
             nc.vector.tensor_reduce(
-                masses[:, first:last],
+                mass[:, first:last],
                 weights[:, first * PAGE : last * PAGE].rearrange("p (g i) -> p g i", i=PAGE),
                 AX.X,
                 ALU.add,
             )
 
-        exponentials(0)
-        nc.vector.tensor_scalar(gap, neg_max[:, 1:2], neg_max[:, 0:1], GAP_CAP, ALU.subtract, ALU.min)
-        exponentials(1)
-        nc.scalar.activation(out=ratio[:], in_=gap, func=ACT.Exp)
-        page_sums(early_mass, 0, HALF_PAGES)
-        page_sums(mass, HALF_PAGES, HALF_PAGES + EARLY_PAGES)
-        nc.vector.tensor_scalar(total[:], sums[:, 0:1], ratio[:], sums[:, 1:2], ALU.mult, ALU.add)
-        page_sums(mass, HALF_PAGES + EARLY_PAGES, PAGES)
-        nc.vector.tensor_scalar(mass[:, :HALF_PAGES], early_mass[:], ratio[:], None, ALU.mult)
-        nc.vector.reciprocal(inverse[:], total[:])
-        nc.vector.tensor_scalar(result[:], mass[:], inverse[:], float(PAGES), ALU.mult, ALU.mult)
+        exponentials(0, HALF_PAGES, neg_max[:, 0:1], stats[:, 6:7])
+        exponentials(HALF_PAGES, 52, neg_shift[:], stats[:, 0:1])
+        exponentials(52, PAGES, neg_shift[:], stats[:, 3:4])
+        page_sums(0, HALF_PAGES)
+        nc.vector.reciprocal(stats[:, 7:8], stats[:, 6:7])
+        page_sums(HALF_PAGES, 52)
+        page_sums(52, PAGES)
+        nc.vector.bn_aggr(inverse[:], stats[:])
+        nc.vector.tensor_scalar(result[:], mass[:], inverse[:, 0:1], float(PAGES), ALU.mult, ALU.mult)
         nc.sync.dma_start(out=out, in_=result[:])

@@ -31,7 +31,7 @@ VECTOR_OF_THIRD = 144
 HALF = SLOTS // 2
 HALF_PAGES = PAGES // 2
 EARLY_PAGES = 8
-GAP_CAP = 64.0
+RATIO_CAP = 2.0**90
 
 
 def tile_attend_headpages_kernel(tc, query, keys, offs, out):
@@ -134,45 +134,51 @@ def tile_attend_headpages_kernel(tc, query, keys, offs, out):
 
         picked = sb.tile([P, SLOTS], F32, name="picked", align_bytes=ALIGN)
         weights = sb.tile([P, SLOTS], F32, name="weights", align_bytes=ALIGN)
-        neg_max = sb.tile([P, 2], F32, name="neg_max")
-        neg_shift = sb.tile([P, 1], F32, name="neg_shift")
-        stats = sb.tile([P, 9], F32, name="stats")
+        early_mass = sb.tile([P, HALF_PAGES], F32, name="early_mass")
+        neg_max1 = sb.tile([P, 1], F32, name="neg_max1")
+        ratio = sb.tile([P, 1], F32, name="ratio")
+        factors = sb.tile([P, 2], F32, name="factors")
+        stats = sb.tile([P, 8], F32, name="stats")
         inverse = sb.tile([P, 2], F32, name="inverse")
         result = sb.tile([P, PAGES], F32, name="result", align_bytes=ALIGN)
         mass = sb.tile([P, PAGES], F32, name="mass", align_bytes=ALIGN)
-        nc.gpsimd.memset(stats[:], 0.0)
+        nc.gpsimd.memset(stats[:, 0:5], 0.0)
+        nc.gpsimd.memset(stats[:, 5:6], float(PAGES))
+        nc.gpsimd.memset(factors[:, 1:2], 1.0)
+        neg_max = [early_mass[:, HALF_PAGES - 1 :], neg_max1[:]]
         halves = [slice(h * HALF, (h + 1) * HALF) for h in range(2)]
         listed = [offsets[:, h * HALF // LIST_ROWS : (h + 1) * HALF // LIST_ROWS] for h in range(2)]
         nc.vector.tensor_copy(picked[:, halves[0]], scores[:].indirect(listed[0]))
         nc.scalar.activation(out=picked[:, halves[1]], in_=scores[:].indirect(listed[1]), func=ACT.Copy)
         for h in range(2):
-            nc.vector.tensor_reduce(neg_max[:, h : h + 1], picked[:, halves[h]], AX.X, ALU.max, negate=True)
-        nc.vector.tensor_scalar(neg_shift[:], neg_max[:, 1:2], GAP_CAP, neg_max[:, 0:1], ALU.add, ALU.min)
+            nc.vector.tensor_reduce(neg_max[h], picked[:, halves[h]], AX.X, ALU.max, negate=True)
 
-        def exponentials(first, last, bias, total):
+        def exponentials(h, total):
             nc.scalar.activation(
-                out=weights[:, first * PAGE : last * PAGE],
-                in_=picked[:, first * PAGE : last * PAGE],
-                func=ACT.Exp,
-                bias=bias,
-                accum_out=total,
+                out=weights[:, halves[h]], in_=picked[:, halves[h]], func=ACT.Exp, bias=neg_max[h], accum_out=total
             )
 
-        def page_sums(first, last):
+        def page_sums(masses, first, last):
             nc.vector.tensor_reduce(
-                mass[:, first:last],
+                masses[:, first:last],
                 weights[:, first * PAGE : last * PAGE].rearrange("p (g i) -> p g i", i=PAGE),
                 AX.X,
                 ALU.add,
             )
 
-        exponentials(0, HALF_PAGES, neg_max[:, 0:1], stats[:, 6:7])
-        exponentials(HALF_PAGES, 52, neg_shift[:], stats[:, 0:1])
-        exponentials(52, PAGES, neg_shift[:], stats[:, 3:4])
-        page_sums(0, HALF_PAGES)
-        nc.vector.reciprocal(stats[:, 7:8], stats[:, 6:7])
-        page_sums(HALF_PAGES, 52)
-        page_sums(52, PAGES)
-        nc.vector.bn_aggr(inverse[:], stats[:])
-        nc.vector.tensor_scalar(result[:], mass[:], inverse[:, 0:1], float(PAGES), ALU.mult, ALU.mult)
+        exponentials(0, factors[:, 0:1])
+        nc.scalar.activation(out=ratio[:], in_=neg_max[0], func=ACT.Exp, scale=-1.0, bias=neg_max[1])
+        exponentials(1, stats[:, 0:1])
+        page_sums(early_mass, 0, 16)
+        nc.vector.scalar_tensor_tensor(
+            stats[:, 3:7:3], ratio[:].to_broadcast([P, 2]), RATIO_CAP, factors[:], ALU.min, ALU.mult
+        )
+        page_sums(early_mass, 16, HALF_PAGES)
+        page_sums(mass, HALF_PAGES, HALF_PAGES + 20)
+        nc.vector.bn_aggr(inverse[:], stats[:, 0:6])
+        page_sums(mass, HALF_PAGES + 20, PAGES)
+        nc.vector.tensor_scalar(
+            result[:, :HALF_PAGES], early_mass[:], stats[:, 6:7], inverse[:, 1:2], ALU.mult, ALU.mult
+        )
+        nc.vector.tensor_scalar(result[:, HALF_PAGES:], mass[:, HALF_PAGES:], inverse[:, 1:2], None, ALU.mult)
         nc.sync.dma_start(out=out, in_=result[:])

from contextlib import ExitStack

import concourse.mybir as mybir

D, T, Q, SLOTS, PAGES = 512, 1024, 128, 512, 64
PAGE = SLOTS // PAGES
FLOPS = 2 * D * T * Q

F32 = mybir.dt.float32
BF16 = mybir.dt.bfloat16
U32 = mybir.dt.uint32
U16 = mybir.dt.uint16
U8 = mybir.dt.uint8
FP8X4 = mybir.dt.float8_e4m3fn_x4
ACT = mybir.ActivationFunctionType
ALU = mybir.AluOpType
AX = mybir.AxisListType

P = 128
PACK = 4
RUN = 4
ALIGN = 256
LIST_ROWS = 16

WIDE, NARROW = 256, 128
LOADS = (WIDE, WIDE, WIDE, NARROW, NARROW)
VECTOR_OF_QUERY, VECTOR_OF_WIDE, VECTOR_OF_FOURTH, VECTOR_OF_LAST = 88, 176, 32, 80
STAGING = slice(384, 896)

VECTOR_OF_THIRD = 144
HALF = SLOTS // 2
HALF_PAGES = PAGES // 2
EARLY_PAGES = 8
RATIO_CAP = 2.0**90


def tile_attend_headpages_kernel(tc, query, keys, offs, out):
    nc = tc.nc
    with ExitStack() as ctx:
        sb = ctx.enter_context(tc.tile_pool(name="sb", bufs=1))
        psum = ctx.enter_context(tc.psum_pool(name="psum", bufs=1))

        scores = sb.tile([P, T], F32, name="scores", align_bytes=ALIGN)

        def staging_tile(name, width):
            return sb.tile([P, PACK, width], F32, name="raw_" + name, align_bytes=ALIGN)[:]

        def load(raw, rows):
            nc.sync.dma_start(out=raw, in_=rows.rearrange("(p j) w -> p j w", j=PACK))
            return raw

        def grouped_tile(name, width):
            return sb.tile([P, width, PACK], BF16, name="grouped_" + name, align_bytes=ALIGN)

        def interleaving_views(grouped, raw, first, last):
            return dict(
                out=grouped[:, first:last, :].rearrange("p (c i) j -> p c j i", i=RUN),
                in_=raw[:, :, first:last].rearrange("p j (c i) -> p c j i", i=RUN),
            )

        def interleave(grouped, raw, vector_cuts):
            for first, last in zip((0,) + vector_cuts, vector_cuts):
                nc.vector.tensor_copy(**interleaving_views(grouped, raw, first, last))
            nc.scalar.activation(func=ACT.Copy, **interleaving_views(grouped, raw, vector_cuts[-1], raw.shape[2]))

        def quantize(name, grouped, first, last, pieces=1):
            width = last - first
            codes = sb.tile([P, width], U32, name="codes_" + name, align_bytes=ALIGN)
            scales = sb.tile([P, width], U8, name="scales_" + name, align_bytes=ALIGN)
            step = width // pieces
            for c in range(0, width, step):
                nc.vector.quantize_mx(
                    out=codes[:, c : c + step].bitcast(FP8X4),
                    scales=scales[:, c : c + step],
                    in_=grouped[:, first + c : first + c + step, :].rearrange("p w j -> p (w j)"),
                )
            return codes, scales

        starts = [sum(LOADS[:n]) for n in range(len(LOADS))]
        q_raw = load(staging_tile("q", Q), query)
        k_raw = [
            load(staging_tile("k%d" % n, w), keys[:, s : s + w])
            for n, (s, w) in enumerate(zip(starts[:-1], LOADS[:-1]))
        ]
        k_raw.append(load(scores[:, STAGING].rearrange("p (j w) -> p j w", j=PACK), keys[:, starts[-1] :]))
        offsets = sb.tile([P, SLOTS // LIST_ROWS], U16, name="offsets")
        nc.sync.dma_start(offsets[:], offs)

        q_grouped = grouped_tile("q", Q)
        interleave(q_grouped, q_raw, (VECTOR_OF_QUERY,))
        q_codes, q_scales = quantize("q", q_grouped, 0, Q)

        k_grouped = [grouped_tile("k%d" % n, w) for n, w in enumerate(LOADS)]

        def multiply(name, n, first, last, pieces=1):
            codes, scales = quantize(name, k_grouped[n], first, last, pieces)
            acc = psum.tile([P, last - first], F32, name="acc_" + name)
            nc.tensor.matmul_mx(
                out=acc[:],
                lhsT=q_codes[:].bitcast(FP8X4),
                lhsT_scale=q_scales[:],
                rhs=codes[:].bitcast(FP8X4),
                rhs_scale=scales[:],
                start=True,
                stop=True,
            )
            return acc, slice(starts[n] + first, starts[n] + last)

        def empty_on_scalar(bank):
            acc, columns = bank
            nc.scalar.activation(out=scores[:, columns], in_=acc[:], func=ACT.Copy)

        def empty_on_vector(bank):
            acc, columns = bank
            nc.vector.tensor_copy(out=scores[:, columns], in_=acc[:])

        def wide_load(n, share):
            interleave(k_grouped[n], k_raw[n], (WIDE // 2, share))
            return multiply("k%d" % n, n, 0, WIDE, pieces=2)

        empty_on_scalar(wide_load(0, VECTOR_OF_WIDE))
        second_bank = wide_load(1, VECTOR_OF_WIDE)
        third_bank = wide_load(2, VECTOR_OF_THIRD)
        interleave(k_grouped[3], k_raw[3], (VECTOR_OF_FOURTH,))
        interleave(k_grouped[4], k_raw[4], (NARROW // 2, VECTOR_OF_LAST))
        fourth_bank = multiply("k3", 3, 0, NARROW)
        fifth_bank = multiply("k4a", 4, 0, NARROW // 2)
        sixth_bank = multiply("k4b", 4, NARROW // 2, NARROW)
        empty_on_scalar(second_bank)
        empty_on_scalar(third_bank)
        empty_on_vector(fourth_bank)
        empty_on_vector(fifth_bank)
        empty_on_scalar(sixth_bank)

        picked = sb.tile([P, SLOTS], F32, name="picked", align_bytes=ALIGN)
        weights = sb.tile([P, SLOTS], F32, name="weights", align_bytes=ALIGN)
        early_mass = sb.tile([P, HALF_PAGES], F32, name="early_mass")
        neg_max1 = sb.tile([P, 1], F32, name="neg_max1")
        ratio = sb.tile([P, 1], F32, name="ratio")
        factors = sb.tile([P, 2], F32, name="factors")
        stats = sb.tile([P, 8], F32, name="stats")
        inverse = sb.tile([P, 2], F32, name="inverse")
        result = sb.tile([P, PAGES], F32, name="result", align_bytes=ALIGN)
        mass = sb.tile([P, PAGES], F32, name="mass", align_bytes=ALIGN)
        nc.gpsimd.memset(stats[:, 0:5], 0.0)
        nc.gpsimd.memset(stats[:, 5:6], float(PAGES))
        nc.gpsimd.memset(factors[:, 1:2], 1.0)
        neg_max = [early_mass[:, HALF_PAGES - 1 :], neg_max1[:]]
        halves = [slice(h * HALF, (h + 1) * HALF) for h in range(2)]
        listed = [offsets[:, h * HALF // LIST_ROWS : (h + 1) * HALF // LIST_ROWS] for h in range(2)]
        nc.vector.tensor_copy(picked[:, halves[0]], scores[:].indirect(listed[0]))
        nc.scalar.activation(out=picked[:, halves[1]], in_=scores[:].indirect(listed[1]), func=ACT.Copy)
        for h in range(2):
            nc.vector.tensor_reduce(neg_max[h], picked[:, halves[h]], AX.X, ALU.max, negate=True)

        def exponentials(h, total):
            nc.scalar.activation(
                out=weights[:, halves[h]], in_=picked[:, halves[h]], func=ACT.Exp, bias=neg_max[h], accum_out=total
            )

        def page_sums(masses, first, last):
            nc.vector.tensor_reduce(
                masses[:, first:last],
                weights[:, first * PAGE : last * PAGE].rearrange("p (g i) -> p g i", i=PAGE),
                AX.X,
                ALU.add,
            )

        exponentials(0, factors[:, 0:1])
        nc.scalar.activation(out=ratio[:], in_=neg_max[0], func=ACT.Exp, scale=-1.0, bias=neg_max[1])
        exponentials(1, stats[:, 0:1])
        page_sums(early_mass, 0, 16)
        nc.vector.scalar_tensor_tensor(
            stats[:, 3:7:3], ratio[:].to_broadcast([P, 2]), RATIO_CAP, factors[:], ALU.min, ALU.mult
        )
        page_sums(early_mass, 16, HALF_PAGES)
        page_sums(mass, HALF_PAGES, HALF_PAGES + 20)
        nc.vector.bn_aggr(inverse[:], stats[:, 0:6])
        page_sums(mass, HALF_PAGES + 20, PAGES)
        nc.vector.tensor_scalar(
            result[:, :HALF_PAGES], early_mass[:], stats[:, 6:7], inverse[:, 1:2], ALU.mult, ALU.mult
        )
        nc.vector.tensor_scalar(result[:, HALF_PAGES:], mass[:, HALF_PAGES:], inverse[:, 1:2], None, ALU.mult)
        nc.sync.dma_start(out=out, in_=result[:])
